import numpy as np
import ml_dtypes


def mxq(x, axis, fmt="e4m3"):
    dtype, down = {"e4m3": (ml_dtypes.float8_e4m3fn, 7), "e5m2": (ml_dtypes.float8_e5m2, 14)}[fmt]
    v = np.moveaxis(np.asarray(x, np.float32).astype(ml_dtypes.bfloat16).astype(np.float64), axis, -1)
    blocks = v.reshape(v.shape[:-1] + (-1, 32))
    amax = np.abs(blocks).max(-1, keepdims=True)
    byte = np.maximum(np.where(amax > 0, np.frexp(amax)[1] - 1 + 127, 0) - down, 1)
    scale = np.exp2(byte - 127.0)
    codes = (blocks / scale).astype(np.float32).astype(dtype).astype(np.float64)
    return np.moveaxis((codes * scale).reshape(v.shape), -1, axis)


WIDE = False


def mx_kscale(k):
    if not WIDE:
        return np.ones(k)
    levels = np.array([10, -10, 5, -5, 0])
    if k % 512:
        return np.exp2(np.random.permutation(np.resize(levels, k // 32))).repeat(32)
    a = np.empty((k // 512, 16))
    for p in range(k // 512):
        a[p, :8] = np.random.permutation(np.resize(levels, 8))
        for g in range(8):
            far = levels[np.abs(levels - a[p, g]) >= 10]
            a[p, g + 8] = far[np.random.randint(len(far))]
    return np.exp2(a.ravel()).repeat(32)


def f64(x):
    return np.asarray(x).astype(np.float64)


def striped(idx):
    return np.tile(idx.reshape(-1, 16).T, (8, 1)).astype(np.uint16)


def unstriped(offs):
    return offs[:16].T.reshape(-1).astype(np.int64)


E2M1 = np.array([0.0, 0.5, 1.0, 1.5, 2.0, 3.0, 4.0, 6.0, -0.0, -0.5, -1.0, -1.5, -2.0, -3.0, -4.0, -6.0])


def pack_weight(w, fmt):
    k, n = w.shape
    w = f64(np.asarray(w, np.float32).astype(ml_dtypes.bfloat16)).reshape(k // 32, 32, n)
    amax = np.abs(w).max(1)
    if fmt == "e4m3":
        byte = np.frexp(amax)[1] - 1 + 127 - 7
    else:
        mant, ex = np.frexp(amax / 6.0)
        byte = np.where(mant > 0.5, ex, ex - 1) + 127
    byte = np.clip(np.where(amax > 0, byte, 1), 1, 254)
    scaled = (w * np.exp2(127.0 - byte)[:, None, :]).reshape(k, n).astype(np.float32)
    by_word = np.ascontiguousarray(scaled.reshape(k // 512, 128, 4, n).transpose(0, 1, 3, 2))
    if fmt == "e4m3":
        words = by_word.astype(ml_dtypes.float8_e4m3fn).view(np.uint8)
    else:
        c = by_word.astype(ml_dtypes.float4_e2m1fn).view(np.uint8) & 0xF
        words = (c[..., 0::2] | (c[..., 1::2] << 4)).reshape(k // 512, 128, 2 * n)
    return np.ascontiguousarray(words), np.ascontiguousarray(byte.astype(np.uint8).reshape(k // 512, 16, n))


def unpack_weight(words, scales, fmt):
    g, _, n = scales.shape
    words = np.ascontiguousarray(words).reshape(g, 128, n, -1)
    if fmt == "e4m3":
        vals = words.view(ml_dtypes.float8_e4m3fn).astype(np.float64)
    else:
        nib = np.empty((g, 128, n, 4), np.uint8)
        nib[..., 0::2] = words & 0xF
        nib[..., 1::2] = words >> 4
        vals = E2M1[nib]
    vals = vals * np.repeat(np.exp2(scales.astype(np.float64) - 127.0), 8, axis=1)[..., None]
    return vals.transpose(0, 1, 3, 2).reshape(g * 512, n)


def pack_table(v):
    words, scales = pack_weight(v, "e4m3")
    return np.concatenate([words.reshape(words.shape[0], -1), scales.reshape(scales.shape[0], -1)], axis=1)


def unpack_table(tab):
    g, t = tab.shape[0], tab.shape[1] // 528
    return unpack_weight(tab[:, :512 * t].reshape(g, 128, t, 4), tab[:, 512 * t:].reshape(g, 16, t), "e4m3")


def split(x):
    m, e = np.frexp(f64(x))
    hi = np.ldexp(np.trunc(16.0 * m) / 16.0, e)
    return hi, f64(x) - hi


K, M, T, S = 1536, 1024, 1024, 256


def setup_inputs():
    n = np.random.standard_normal
    s = mx_kscale(K)[:, None]
    return {
        "tab": pack_table(n((K, T)) * s),
        "w": (n((K, M)) / np.sqrt(K) / s).astype(np.float32),
        "b": (0.3 * n(1024)).astype(np.float32),
        "offs": striped(np.random.permutation(T)[:S]),
    }


def reference(tab, w, b, offs):
    tab_ = unpack_table(tab)[:, unstriped(offs)]
    w_hi, w_lo = split(w)
    w_hi_, w_lo_ = mxq(w_hi, 0, "e4m3"), mxq(w_lo, 0, "e4m3")
    y = tab_.T @ w_hi_ + tab_.T @ w_lo_
    return y + f64(b)[None, :]

@@ -1,0 +1,202 @@
+from contextlib import ExitStack
+
+import concourse.mybir as mybir
+
+K, M, T, S = 1536, 1024, 1024, 256
+
+F32 = mybir.dt.float32
+BF16 = mybir.dt.bfloat16
+I32 = mybir.dt.int32
+U32 = mybir.dt.uint32
+U16 = mybir.dt.uint16
+U8 = mybir.dt.uint8
+FP8X4 = mybir.dt.float8_e4m3fn_x4
+ADD = mybir.AluOpType.add
+SUB = mybir.AluOpType.subtract
+AND = mybir.AluOpType.bitwise_and
+
+FLOPS = 2 * 2 * S * K * M
+
+P = 128
+PACK = 4
+PASSES = 3
+HALF = 512
+MASK32 = -0x00100000
+MASK = -0x000F0010
+
+
+def tile_list_tabw_tm_hl_bias_kernel(tc, tab, w, b, offs, out):
+    nc = tc.nc
+    with ExitStack() as ctx:
+        lists = ctx.enter_context(tc.tile_pool(name="lists", bufs=1))
+        keep = ctx.enter_context(tc.tile_pool(name="keep", bufs=1))
+        psum = ctx.enter_context(tc.psum_pool(name="psum", bufs=1))
+
+        offsets = lists.tile([P, S // 16], U16, name="offsets")
+        words = [keep.tile([P, T], I32, name="words%d" % a, align_bytes=64) for a in range(PASSES)]
+        planes = keep.tile([P, T // 4], I32, name="planes", align_bytes=64)
+        g_words = [keep.tile([P, S], U32, name="gwords%d" % a, align_bytes=64) for a in range(PASSES)]
+        g_planes = keep.tile([P, S], U8, name="gplanes", align_bytes=64)
+        bias = keep.tile([P, M], F32, name="bias", align_bytes=64)
+
+        pieces = [
+            (0, 0, 0, 128), (0, 0, 128, 128), (0, 0, 256, 256),
+            (0, 1, 0, 256), (0, 1, 256, 256), (0, 2, 0, 512),
+            (1, 0, 0, 512), (1, 1, 0, 512), (1, 2, 0, 256), (1, 2, 256, 128), (1, 2, 384, 128),
+        ]
+        raw = {}
+        top = {}
+        hi = {}
+        lo = {}
+        codes = {}
+        scales = {}
+        for pc in pieces:
+            h, a, c0, wd = pc
+            tagname = "%d_%d_%d" % (h, a, c0)
+            raw[pc] = keep.tile([P, PACK, wd], F32, name="raw" + tagname, align_bytes=64)
+            top[pc] = keep.tile([P, wd, PACK], BF16, name="top" + tagname, align_bytes=64)
+            hi[pc] = keep.tile([P, wd, PACK], BF16, name="hi" + tagname, align_bytes=64)
+            lo[pc] = keep.tile([P, wd, PACK], BF16, name="lo" + tagname, align_bytes=64)
+        for h in range(2):
+            for a in range(PASSES):
+                for part in ("hi", "lo"):
+                    codes[h, a, part] = keep.tile([P, HALF], U32, name="codes_%s%d%d" % (part, h, a), align_bytes=64)
+                    scales[h, a, part] = keep.tile([P, HALF], U8, name="scales_%s%d%d" % (part, h, a), align_bytes=64)
+
+        def load_w(pc):
+            h, a, c0, wd = pc
+            n0 = h * HALF + c0
+            src = w[512 * a : 512 * (a + 1), n0 : n0 + wd].rearrange("(p j) n -> p j n", j=PACK)
+            nc.sync.dma_start(raw[pc][:], src)
+
+        def load_words(a):
+            src = tab[a : a + 1, 0 : 512 * T].rearrange("o (p x) -> (o p) x", p=P).bitcast(I32)
+            nc.sync.dma_start(words[a][:], src)
+
+        warm = keep.tile([P, 2], BF16, name="warm")
+        nc.gpsimd.memset(warm[:], 0)
+        nc.scalar.copy(warm[:, 1:2], warm[:, 0:1])
+        nc.vector.memset(planes[:], 0)
+        nc.sync.dma_start(offsets[:], offs)
+        for q in range(4):
+            first = 512 * T + 4 * q * T
+            src = tab[:, first : first + 4 * T].rearrange("a (r t) -> a r t", r=4).bitcast(I32)
+            nc.scalar.dma_start(planes[32 * q : 32 * q + 4 * PASSES, :], src)
+        for i in range(4):
+            load_w(pieces[i])
+        load_words(0)
+        load_w(pieces[4])
+        load_words(1)
+        load_words(2)
+        load_w(pieces[5])
+        nc.sync.dma_start(bias[:], b.partition_broadcast(P))
+        for pc in pieces[6:]:
+            load_w(pc)
+
+        hi32 = keep.tile([P, PACK, 128], F32, name="hi32", align_bytes=64)
+        nc.vector.tensor_copy(g_planes[:], planes[:].bitcast(U8).indirect(offsets[:]))
+        nc.vector.tensor_single_scalar(hi32[:].bitcast(I32), raw[pieces[0]][:].bitcast(I32), MASK32, AND)
+        nc.scalar.copy(hi[pieces[0]][:].rearrange("p (c i) j -> p c j i", i=4), hi32[:].rearrange("p j (c i) -> p c j i", i=4))
+        for pc in pieces[1:]:
+            src = raw[pc][:].bitcast(BF16).rearrange("p j (c i u) -> p c j i u", i=4, u=2)
+            dst = top[pc][:].rearrange("p (c i) j -> p c j i", i=4)
+            nc.scalar.copy(dst, src[:, :, :, :, 1])
+
+        def mask_hi(pc):
+            nc.vector.tensor_single_scalar(
+                hi[pc][:].rearrange("p n j -> p (n j)").bitcast(I32),
+                top[pc][:].rearrange("p n j -> p (n j)").bitcast(I32),
+                MASK,
+                AND,
+            )
+
+        def sub_lo(pc):
+            nc.vector.tensor_tensor(
+                lo[pc][:].rearrange("p (c i) j -> p c j i", i=4),
+                raw[pc][:].rearrange("p j (c i) -> p c j i", i=4),
+                hi32[:].rearrange("p j (c i) -> p c j i", i=4) if pc == pieces[0] else hi[pc][:].rearrange("p (c i) j -> p c j i", i=4),
+                SUB,
+            )
+
+        def quant(pc, part):
+            h, a, c0, wd = pc
+            src = hi[pc] if part == "hi" else lo[pc]
+            nc.vector.quantize_mx(
+                out=codes[h, a, part][:, c0 : c0 + wd].bitcast(FP8X4),
+                scales=scales[h, a, part][:, c0 : c0 + wd],
+                in_=src[:].rearrange("p n j -> p (n j)"),
+            )
+
+        def gather_words(a):
+            nc.vector.tensor_copy(g_words[a][:], words[a][:].bitcast(U32).indirect(offsets[:]))
+
+        acc = {}
+        for j in range(2):
+            acc[j, 0, 0] = psum.tile([P, 512], F32, name="acc%d0" % j)
+            acc[j, 1, 0] = psum.tile([P, 256], F32, name="acc%d1a" % j)
+            acc[j, 1, 256] = psum.tile([P, 128], F32, name="acc%d1b" % j)
+            acc[j, 1, 384] = psum.tile([P, 128], F32, name="acc%d1c" % j)
+
+        def multiply(h, a, part, c0, wd):
+            for j in range(2):
+                nc.tensor.matmul_mx(
+                    out=acc[j, h, c0][:],
+                    lhsT=g_words[a][:, 128 * j : 128 * (j + 1)].bitcast(FP8X4),
+                    lhsT_scale=g_planes[4 * a : P, 128 * j : 128 * (j + 1)],
+                    rhs=codes[h, a, part][:, c0 : c0 + wd].bitcast(FP8X4),
+                    rhs_scale=scales[h, a, part][:, c0 : c0 + wd],
+                    start=(a == 0 and part == "hi"),
+                    stop=(a == PASSES - 1 and part == "lo"),
+                )
+
+        def finish(h, c0, wd):
+            n0 = h * HALF + c0
+            for j in range(2):
+                y = keep.tile([P, wd], F32, name="y%d_%d_%d" % (h, c0, j), align_bytes=64)
+                nc.vector.tensor_tensor(y[:], acc[j, h, c0][:], bias[:, n0 : n0 + wd], ADD)
+                (nc.scalar if j == 1 and c0 == 384 else nc.sync).dma_start(out[128 * j : 128 * (j + 1), n0 : n0 + wd], y[:])
+
+        def mult_piece(i, part):
+            h, a, c0, wd = pieces[i]
+            if h == 0:
+                if c0 + wd == HALF:
+                    if a in gathered:
+                        multiply(0, a, part, 0, HALF)
+                    else:
+                        pending.append((0, a, part, 0, HALF))
+            else:
+                for c, cw in ((0, 256), (256, 128), (384, 128)):
+                    if c0 <= c < c0 + wd:
+                        multiply(1, a, part, c, cw)
+
+        gathers = {3: 0, 4: 1, 5: 2}
+        pending = []
+        gathered = []
+        n = len(pieces)
+        for i in range(n):
+            if i > 0:
+                mask_hi(pieces[i])
+                if i > 1:
+                    quant(pieces[i - 1], "lo")
+                    mult_piece(i - 1, "lo")
+            if i in gathers:
+                gather_words(gathers[i])
+                gathered.append(gathers[i])
+                for args in pending:
+                    multiply(*args)
+                pending.clear()
+            if i == 7:
+                finish(0, 0, 512)
+            sub_lo(pieces[i])
+            if i > 0:
+                quant(pieces[i], "hi")
+                mult_piece(i, "hi")
+            if i == 1:
+                quant(pieces[0], "hi")
+                quant(pieces[0], "lo")
+            if i == n - 1:
+                finish(1, 0, 256)
+        quant(pieces[n - 1], "lo")
+        mult_piece(n - 1, "lo")
+        finish(1, 256, 128)
+        finish(1, 384, 128)

@@ -76,12 +76,12 @@ def tile_list_tabw_tm_hl_bias_kernel(tc, tab, w, b, offs, out):
         warm = keep.tile([P, 2], BF16, name="warm")
         nc.gpsimd.memset(warm[:], 0)
         nc.scalar.copy(warm[:, 1:2], warm[:, 0:1])
-        nc.vector.memset(planes[:], 0)
+        nc.gpsimd.memset(planes[:], 0)
         nc.sync.dma_start(offsets[:], offs)
         for q in range(4):
             first = 512 * T + 4 * q * T
             src = tab[:, first : first + 4 * T].rearrange("a (r t) -> a r t", r=4).bitcast(I32)
-            nc.scalar.dma_start(planes[32 * q : 32 * q + 4 * PASSES, :], src)
+            nc.gpsimd.dma_start(planes[32 * q : 32 * q + 4 * PASSES, :], src)
         for i in range(4):
             load_w(pieces[i])
         load_words(0)
@@ -89,18 +89,19 @@ def tile_list_tabw_tm_hl_bias_kernel(tc, tab, w, b, offs, out):
         load_words(1)
         load_words(2)
         load_w(pieces[5])
-        nc.sync.dma_start(bias[:], b.partition_broadcast(P))
         for pc in pieces[6:]:
             load_w(pc)
+        nc.sync.dma_start(bias[:], b.partition_broadcast(P))
 
         hi32 = keep.tile([P, PACK, 128], F32, name="hi32", align_bytes=64)
-        nc.vector.tensor_copy(g_planes[:], planes[:].bitcast(U8).indirect(offsets[:]))
         nc.vector.tensor_single_scalar(hi32[:].bitcast(I32), raw[pieces[0]][:].bitcast(I32), MASK32, AND)
         nc.scalar.copy(hi[pieces[0]][:].rearrange("p (c i) j -> p c j i", i=4), hi32[:].rearrange("p j (c i) -> p c j i", i=4))
         for pc in pieces[1:]:
             src = raw[pc][:].bitcast(BF16).rearrange("p j (c i u) -> p c j i u", i=4, u=2)
             dst = top[pc][:].rearrange("p (c i) j -> p c j i", i=4)
-            nc.scalar.copy(dst, src[:, :, :, :, 1])
+            step = min(64, pc[3] // 4)
+            for c in range(0, pc[3] // 4, step):
+                nc.scalar.copy(dst[:, c : c + step], src[:, c : c + step, :, :, 1])
 
         def mask_hi(pc):
             nc.vector.tensor_single_scalar(
@@ -185,7 +186,9 @@ def tile_list_tabw_tm_hl_bias_kernel(tc, tab, w, b, offs, out):
                 for args in pending:
                     multiply(*args)
                 pending.clear()
-            if i == 7:
+            if i == 2:
+                nc.vector.tensor_copy(g_planes[:], planes[:].bitcast(U8).indirect(offsets[:]))
+            if i == 8:
                 finish(0, 0, 512)
             sub_lo(pieces[i])
             if i > 0:

@@ -1,6 +1,7 @@
 from contextlib import ExitStack
 
 import concourse.mybir as mybir
+from concourse.masks import make_identity
 
 K, M, T, S = 1536, 1024, 1024, 256
 
@@ -37,7 +38,7 @@ def tile_list_tabw_tm_hl_bias_kernel(tc, tab, w, b, offs, out):
         planes = keep.tile([P, T // 4], I32, name="planes", align_bytes=64)
         g_words = [keep.tile([P, S], U32, name="gwords%d" % a, align_bytes=64) for a in range(PASSES)]
         g_planes = keep.tile([P, S], U8, name="gplanes", align_bytes=64)
-        bias = keep.tile([P, M], F32, name="bias", align_bytes=64)
+        bias = keep.tile([P, 256], F32, name="bias", align_bytes=64)
 
         pieces = [
             (0, 0, 0, 128), (0, 0, 128, 128), (0, 0, 256, 256),
@@ -76,12 +77,13 @@ def tile_list_tabw_tm_hl_bias_kernel(tc, tab, w, b, offs, out):
         warm = keep.tile([P, 2], BF16, name="warm")
         nc.gpsimd.memset(warm[:], 0)
         nc.scalar.copy(warm[:, 1:2], warm[:, 0:1])
-        nc.gpsimd.memset(planes[:], 0)
+        nc.vector.memset(planes[:], 0)
         nc.sync.dma_start(offsets[:], offs)
-        for q in range(4):
-            first = 512 * T + 4 * q * T
-            src = tab[:, first : first + 4 * T].rearrange("a (r t) -> a r t", r=4).bitcast(I32)
-            nc.gpsimd.dma_start(planes[32 * q : 32 * q + 4 * PASSES, :], src)
+        for a0, a1 in ((0, 2), (2, 3)):
+            for q in range(4):
+                first = 512 * T + 4 * q * T
+                src = tab[a0:a1, first : first + 4 * T].rearrange("a (r t) -> a r t", r=4).bitcast(I32)
+                nc.scalar.dma_start(planes[32 * q + 4 * a0 : 32 * q + 4 * a1, :], src)
         for i in range(4):
             load_w(pieces[i])
         load_words(0)
@@ -91,7 +93,11 @@ def tile_list_tabw_tm_hl_bias_kernel(tc, tab, w, b, offs, out):
         load_w(pieces[5])
         for pc in pieces[6:]:
             load_w(pc)
-        nc.sync.dma_start(bias[:], b.partition_broadcast(P))
+        b_col = keep.tile([P, 6], F32, name="bcol")
+        nc.sync.dma_start(b_col[:], b[0:768].rearrange("(c p) -> p c", p=P))
+        nc.sync.dma_start(bias[:], b[768:1024].partition_broadcast(P))
+        ident = keep.tile([P, P], F32, name="ident", align_bytes=64)
+        make_identity(nc, ident[:])
 
         hi32 = keep.tile([P, PACK, 128], F32, name="hi32", align_bytes=64)
         nc.vector.tensor_single_scalar(hi32[:].bitcast(I32), raw[pieces[0]][:].bitcast(I32), MASK32, AND)
@@ -131,48 +137,86 @@ def tile_list_tabw_tm_hl_bias_kernel(tc, tab, w, b, offs, out):
         def gather_words(a):
             nc.vector.tensor_copy(g_words[a][:], words[a][:].bitcast(U32).indirect(offsets[:]))
 
-        acc = {}
+        acc_n = {}
+        acc_j = {}
+        for t in range(4):
+            acc_n[t] = psum.tile([P, S], F32, name="bank%d" % t, tag="bank%d" % t)
         for j in range(2):
-            acc[j, 0, 0] = psum.tile([P, 512], F32, name="acc%d0" % j)
-            acc[j, 1, 0] = psum.tile([P, 256], F32, name="acc%d1a" % j)
-            acc[j, 1, 256] = psum.tile([P, 128], F32, name="acc%d1b" % j)
-            acc[j, 1, 384] = psum.tile([P, 128], F32, name="acc%d1c" % j)
+            for c in range(2):
+                acc_j[j, c] = psum.tile([P, 128], F32, name="accj%d%d" % (j, c))
 
-        def multiply(h, a, part, c0, wd):
+        def mult_n(t, a, part):
+            h, c = t // 4, 128 * (t % 4)
+            nc.tensor.matmul_mx(
+                out=acc_n[t][:],
+                lhsT=codes[h, a, part][:, c : c + 128].bitcast(FP8X4),
+                lhsT_scale=scales[h, a, part][:, c : c + 128],
+                rhs=g_words[a][:].bitcast(FP8X4),
+                rhs_scale=g_planes[4 * a : P, :],
+                start=(a == 0 and part == "hi"),
+                stop=(a == PASSES - 1 and part == "lo"),
+            )
+
+        def mult_j(c, a, part):
             for j in range(2):
                 nc.tensor.matmul_mx(
-                    out=acc[j, h, c0][:],
+                    out=acc_j[j, c][:],
                     lhsT=g_words[a][:, 128 * j : 128 * (j + 1)].bitcast(FP8X4),
                     lhsT_scale=g_planes[4 * a : P, 128 * j : 128 * (j + 1)],
-                    rhs=codes[h, a, part][:, c0 : c0 + wd].bitcast(FP8X4),
-                    rhs_scale=scales[h, a, part][:, c0 : c0 + wd],
+                    rhs=codes[1, a, part][:, 256 + 128 * c : 384 + 128 * c].bitcast(FP8X4),
+                    rhs_scale=scales[1, a, part][:, 256 + 128 * c : 384 + 128 * c],
                     start=(a == 0 and part == "hi"),
                     stop=(a == PASSES - 1 and part == "lo"),
                 )
 
-        def finish(h, c0, wd):
-            n0 = h * HALF + c0
+        def finish_n(t0, t1):
+            yt = {}
+            for t in range(t0, t1):
+                yt[t] = keep.tile([P, S], F32, name="yt%d" % t, align_bytes=64)
+                nc.scalar.activation(yt[t][:], acc_n[t][:], mybir.ActivationFunctionType.Identity, bias=b_col[:, t : t + 1])
+            n = 128 * (t1 - t0)
             for j in range(2):
-                y = keep.tile([P, wd], F32, name="y%d_%d_%d" % (h, c0, j), align_bytes=64)
-                nc.vector.tensor_tensor(y[:], acc[j, h, c0][:], bias[:, n0 : n0 + wd], ADD)
-                (nc.scalar if j == 1 and c0 == 384 else nc.sync).dma_start(out[128 * j : 128 * (j + 1), n0 : n0 + wd], y[:])
+                turned = psum.tile([P, n], F32, name="turned%d_%d" % (t0, j), tag="bank%d" % j)
+                for t in range(t0, t1):
+                    nc.tensor.transpose(turned[:, 128 * (t - t0) : 128 * (t - t0 + 1)], yt[t][:, 128 * j : 128 * (j + 1)], ident[:])
+                y = keep.tile([P, n], F32, name="y%d_%d" % (t0, j), align_bytes=64)
+                nc.scalar.copy(y[:], turned[:])
+                nc.sync.dma_start(out[128 * j : 128 * (j + 1), 128 * t0 : 128 * t1], y[:])
+
+        def finish_j(c):
+            n0 = 768 + 128 * c
+            for j in range(2):
+                y = keep.tile([P, 128], F32, name="yj%d_%d" % (c, j), align_bytes=64)
+                nc.vector.tensor_tensor(y[:], acc_j[j, c][:], bias[:, 128 * c : 128 * (c + 1)], ADD)
+                (nc.scalar if j == 1 else nc.sync).dma_start(out[128 * j : 128 * (j + 1), n0 : n0 + 128], y[:])
+
+        pending = []
+        state = {"gathered": [], "first": False}
+
+        def ready(job):
+            kind, where, a, part = job
+            return a in state["gathered"] and (kind == "j" or where < 4 or state["first"])
+
+        def flush():
+            todo = list(pending)
+            pending.clear()
+            for job in todo:
+                if ready(job):
+                    if job[0] == "n":
+                        mult_n(job[1], job[2], job[3])
+                    else:
+                        mult_j(job[1], job[2], job[3])
+                else:
+                    pending.append(job)
 
         def mult_piece(i, part):
             h, a, c0, wd = pieces[i]
-            if h == 0:
-                if c0 + wd == HALF:
-                    if a in gathered:
-                        multiply(0, a, part, 0, HALF)
-                    else:
-                        pending.append((0, a, part, 0, HALF))
-            else:
-                for c, cw in ((0, 256), (256, 128), (384, 128)):
-                    if c0 <= c < c0 + wd:
-                        multiply(1, a, part, c, cw)
+            for c in range(c0, c0 + wd, 128):
+                n0 = h * HALF + c
+                pending.append(("n", n0 // 128, a, part) if n0 < 768 else ("j", n0 // 128 - 6, a, part))
+            flush()
 
         gathers = {3: 0, 4: 1, 5: 2}
-        pending = []
-        gathered = []
         n = len(pieces)
         for i in range(n):
             if i > 0:
@@ -182,24 +226,29 @@ def tile_list_tabw_tm_hl_bias_kernel(tc, tab, w, b, offs, out):
                     mult_piece(i - 1, "lo")
             if i in gathers:
                 gather_words(gathers[i])
-                gathered.append(gathers[i])
-                for args in pending:
-                    multiply(*args)
-                pending.clear()
+                state["gathered"].append(gathers[i])
+                flush()
             if i == 2:
                 nc.vector.tensor_copy(g_planes[:], planes[:].bitcast(U8).indirect(offsets[:]))
-            if i == 8:
-                finish(0, 0, 512)
+            if i == 7:
+                finish_n(0, 4)
+                for t in (4, 5):
+                    acc_n[t] = psum.tile([P, S], F32, name="bank_%d" % t, tag="bank%d" % (t - 2))
+                state["first"] = True
+                flush()
+            if i == 9:
+                finish_n(4, 6)
             sub_lo(pieces[i])
             if i > 0:
                 quant(pieces[i], "hi")
                 mult_piece(i, "hi")
             if i == 1:
                 quant(pieces[0], "hi")
+                mult_piece(0, "hi")
                 quant(pieces[0], "lo")
+                mult_piece(0, "lo")
             if i == n - 1:
-                finish(1, 0, 256)
+                finish_j(0)
         quant(pieces[n - 1], "lo")
         mult_piece(n - 1, "lo")
-        finish(1, 256, 128)
-        finish(1, 384, 128)
+        finish_j(1)

@@ -15,6 +15,7 @@ FP8X4 = mybir.dt.float8_e4m3fn_x4
 ADD = mybir.AluOpType.add
 SUB = mybir.AluOpType.subtract
 AND = mybir.AluOpType.bitwise_and
+IDENTITY = mybir.ActivationFunctionType.Identity
 
 FLOPS = 2 * 2 * S * K * M
 
@@ -23,7 +24,7 @@ PACK = 4
 PASSES = 3
 HALF = 512
 MASK32 = -0x00100000
-MASK = -0x000F0010
+MASK16 = -0x000F0010
 
 
 def tile_list_tabw_tm_hl_bias_kernel(tc, tab, w, b, offs, out):
@@ -39,103 +40,114 @@ def tile_list_tabw_tm_hl_bias_kernel(tc, tab, w, b, offs, out):
         g_words = [keep.tile([P, S], U32, name="gwords%d" % a, align_bytes=64) for a in range(PASSES)]
         g_planes = keep.tile([P, S], U8, name="gplanes", align_bytes=64)
         bias = keep.tile([P, 256], F32, name="bias", align_bytes=64)
+        b_col = keep.tile([P, 6], F32, name="bcol")
+        ident = keep.tile([P, P], F32, name="ident", align_bytes=64)
 
+        loads = [(0, 0, 128), (0, 128, 128), (0, 256, 256), (1, 0, 512), (2, 0, 512), (0, 512, 512), (1, 512, 512), (2, 512, 512)]
         pieces = [
-            (0, 0, 0, 128), (0, 0, 128, 128), (0, 0, 256, 256),
-            (0, 1, 0, 256), (0, 1, 256, 256), (0, 2, 0, 512),
-            (1, 0, 0, 512), (1, 1, 0, 512), (1, 2, 0, 256), (1, 2, 256, 128), (1, 2, 384, 128),
+            (0, 0, 128, True), (1, 0, 128, False), (2, 0, 256, True), (3, 0, 256, False), (3, 256, 256, False), (4, 0, 512, False),
+            (5, 0, 512, False), (6, 0, 512, False), (7, 0, 256, False), (7, 256, 128, False), (7, 384, 128, False),
         ]
-        raw = {}
-        top = {}
-        hi = {}
-        lo = {}
+        raw = [keep.tile([P, PACK, wd], F32, name="raw%d" % i, align_bytes=64) for i, (a, c, wd) in enumerate(loads)]
+        top = [keep.tile([P, wd, PACK], BF16, name="top%d" % i, align_bytes=64) for i, (ld, c, wd, wide) in enumerate(pieces)]
+        hi = [keep.tile([P, wd, PACK], BF16, name="hi%d" % i, align_bytes=64) for i, (ld, c, wd, wide) in enumerate(pieces)]
+        lo = [keep.tile([P, wd, PACK], BF16, name="lo%d" % i, align_bytes=64) for i, (ld, c, wd, wide) in enumerate(pieces)]
         codes = {}
         scales = {}
-        for pc in pieces:
-            h, a, c0, wd = pc
-            tagname = "%d_%d_%d" % (h, a, c0)
-            raw[pc] = keep.tile([P, PACK, wd], F32, name="raw" + tagname, align_bytes=64)
-            top[pc] = keep.tile([P, wd, PACK], BF16, name="top" + tagname, align_bytes=64)
-            hi[pc] = keep.tile([P, wd, PACK], BF16, name="hi" + tagname, align_bytes=64)
-            lo[pc] = keep.tile([P, wd, PACK], BF16, name="lo" + tagname, align_bytes=64)
         for h in range(2):
             for a in range(PASSES):
                 for part in ("hi", "lo"):
                     codes[h, a, part] = keep.tile([P, HALF], U32, name="codes_%s%d%d" % (part, h, a), align_bytes=64)
                     scales[h, a, part] = keep.tile([P, HALF], U8, name="scales_%s%d%d" % (part, h, a), align_bytes=64)
 
-        def load_w(pc):
-            h, a, c0, wd = pc
-            n0 = h * HALF + c0
-            src = w[512 * a : 512 * (a + 1), n0 : n0 + wd].rearrange("(p j) n -> p j n", j=PACK)
-            nc.sync.dma_start(raw[pc][:], src)
+        def load_w(i):
+            a, c, wd = loads[i]
+            nc.sync.dma_start(raw[i][:], w[512 * a : 512 * (a + 1), c : c + wd].rearrange("(p j) n -> p j n", j=PACK))
 
         def load_words(a):
-            src = tab[a : a + 1, 0 : 512 * T].rearrange("o (p x) -> (o p) x", p=P).bitcast(I32)
-            nc.sync.dma_start(words[a][:], src)
+            nc.sync.dma_start(words[a][:], tab[a : a + 1, 0 : 512 * T].rearrange("o (p x) -> (o p) x", p=P).bitcast(I32))
 
         warm = keep.tile([P, 2], BF16, name="warm")
         nc.gpsimd.memset(warm[:], 0)
         nc.scalar.copy(warm[:, 1:2], warm[:, 0:1])
         nc.vector.memset(planes[:], 0)
+        load_w(0)
+        load_w(1)
         nc.sync.dma_start(offsets[:], offs)
-        for a0, a1 in ((0, 2), (2, 3)):
-            for q in range(4):
-                first = 512 * T + 4 * q * T
-                src = tab[a0:a1, first : first + 4 * T].rearrange("a (r t) -> a r t", r=4).bitcast(I32)
-                nc.scalar.dma_start(planes[32 * q + 4 * a0 : 32 * q + 4 * a1, :], src)
-        for i in range(4):
-            load_w(pieces[i])
+        load_w(2)
+        for q in range(4):
+            first = 512 * T + 4 * q * T
+            src = tab[:, first : first + 4 * T].rearrange("a (r t) -> a r t", r=4).bitcast(I32)
+            nc.sync.dma_start(planes[32 * q : 32 * q + 4 * PASSES, :], src)
+        load_w(3)
         load_words(0)
-        load_w(pieces[4])
+        load_w(4)
         load_words(1)
+        load_w(5)
         load_words(2)
-        load_w(pieces[5])
-        for pc in pieces[6:]:
-            load_w(pc)
-        b_col = keep.tile([P, 6], F32, name="bcol")
+        load_w(6)
+        load_w(7)
         nc.sync.dma_start(b_col[:], b[0:768].rearrange("(c p) -> p c", p=P))
         nc.sync.dma_start(bias[:], b[768:1024].partition_broadcast(P))
-        ident = keep.tile([P, P], F32, name="ident", align_bytes=64)
         make_identity(nc, ident[:])
 
-        hi32 = keep.tile([P, PACK, 128], F32, name="hi32", align_bytes=64)
-        nc.vector.tensor_single_scalar(hi32[:].bitcast(I32), raw[pieces[0]][:].bitcast(I32), MASK32, AND)
-        nc.scalar.copy(hi[pieces[0]][:].rearrange("p (c i) j -> p c j i", i=4), hi32[:].rearrange("p j (c i) -> p c j i", i=4))
-        for pc in pieces[1:]:
-            src = raw[pc][:].bitcast(BF16).rearrange("p j (c i u) -> p c j i u", i=4, u=2)
-            dst = top[pc][:].rearrange("p (c i) j -> p c j i", i=4)
-            step = min(64, pc[3] // 4)
-            for c in range(0, pc[3] // 4, step):
-                nc.scalar.copy(dst[:, c : c + step], src[:, c : c + step, :, :, 1])
+        def columns(i):
+            ld, c, wd, wide = pieces[i]
+            return raw[ld][:, :, c : c + wd]
 
-        def mask_hi(pc):
-            nc.vector.tensor_single_scalar(
-                hi[pc][:].rearrange("p n j -> p (n j)").bitcast(I32),
-                top[pc][:].rearrange("p n j -> p (n j)").bitcast(I32),
-                MASK,
-                AND,
-            )
+        def by_four(tile):
+            return tile.rearrange("p (c i) j -> p c j i", i=4)
 
-        def sub_lo(pc):
-            nc.vector.tensor_tensor(
-                lo[pc][:].rearrange("p (c i) j -> p c j i", i=4),
-                raw[pc][:].rearrange("p j (c i) -> p c j i", i=4),
-                hi32[:].rearrange("p j (c i) -> p c j i", i=4) if pc == pieces[0] else hi[pc][:].rearrange("p (c i) j -> p c j i", i=4),
-                SUB,
-            )
+        wides = {}
+        for i, (ld, c, wd, wide) in enumerate(pieces):
+            if wide:
+                wides[i] = keep.tile([P, PACK, wd], F32, name="wide%d" % i, align_bytes=64)
 
-        def quant(pc, part):
-            h, a, c0, wd = pc
-            src = hi[pc] if part == "hi" else lo[pc]
+        def mask_hi(i):
+            if i in wides:
+                nc.vector.tensor_single_scalar(wides[i][:].bitcast(I32), columns(i).bitcast(I32), MASK32, AND)
+                nc.scalar.copy(by_four(hi[i][:]), wides[i][:].rearrange("p j (c i) -> p c j i", i=4))
+            else:
+                nc.vector.tensor_single_scalar(
+                    hi[i][:].rearrange("p n j -> p (n j)").bitcast(I32),
+                    top[i][:].rearrange("p n j -> p (n j)").bitcast(I32),
+                    MASK16,
+                    AND,
+                )
+
+        def copy_top(i):
+            ld, c0, wd, wide = pieces[i]
+            if not wide:
+                src = raw[ld][:].bitcast(BF16).rearrange("p j (c i u) -> p c j i u", i=4, u=2)
+                dst = by_four(top[i][:])
+                step = min(64, wd // 4)
+                for c in range(0, wd // 4, step):
+                    nc.scalar.copy(dst[:, c : c + step], src[:, c0 // 4 + c : c0 // 4 + c + step, :, :, 1])
+
+        def sub_lo(i):
+            high = wides[i][:].rearrange("p j (c i) -> p c j i", i=4) if i in wides else by_four(hi[i][:])
+            nc.vector.tensor_tensor(by_four(lo[i][:]), columns(i).rearrange("p j (c i) -> p c j i", i=4), high, SUB)
+
+        def place(i):
+            ld, c, wd, wide = pieces[i]
+            a, n0, lw = loads[ld]
+            return a, n0 + c, wd
+
+        def quant(i, part):
+            a, n0, wd = place(i)
+            h, c = divmod(n0, HALF)
+            src = hi[i] if part == "hi" else lo[i]
             nc.vector.quantize_mx(
-                out=codes[h, a, part][:, c0 : c0 + wd].bitcast(FP8X4),
-                scales=scales[h, a, part][:, c0 : c0 + wd],
+                out=codes[h, a, part][:, c : c + wd].bitcast(FP8X4),
+                scales=scales[h, a, part][:, c : c + wd],
                 in_=src[:].rearrange("p n j -> p (n j)"),
             )
+            for n in range(n0, n0 + wd, 128):
+                pending.append((n // 128, a, part))
 
         def gather_words(a):
             nc.vector.tensor_copy(g_words[a][:], words[a][:].bitcast(U32).indirect(offsets[:]))
+            gathered.append(a)
 
         acc_n = {}
         acc_j = {}
@@ -145,35 +157,44 @@ def tile_list_tabw_tm_hl_bias_kernel(tc, tab, w, b, offs, out):
             for c in range(2):
                 acc_j[j, c] = psum.tile([P, 128], F32, name="accj%d%d" % (j, c))
 
-        def mult_n(t, a, part):
-            h, c = t // 4, 128 * (t % 4)
-            nc.tensor.matmul_mx(
-                out=acc_n[t][:],
-                lhsT=codes[h, a, part][:, c : c + 128].bitcast(FP8X4),
-                lhsT_scale=scales[h, a, part][:, c : c + 128],
-                rhs=g_words[a][:].bitcast(FP8X4),
-                rhs_scale=g_planes[4 * a : P, :],
-                start=(a == 0 and part == "hi"),
-                stop=(a == PASSES - 1 and part == "lo"),
-            )
+        pending = []
+        gathered = []
 
-        def mult_j(c, a, part):
-            for j in range(2):
+        def multiply(t, a, part):
+            h, c = t // 4, 128 * (t % 4)
+            cols = codes[h, a, part][:, c : c + 128].bitcast(FP8X4)
+            col_scales = scales[h, a, part][:, c : c + 128]
+            start = a == 0 and part == "hi"
+            stop = a == PASSES - 1 and part == "lo"
+            if t < 6:
                 nc.tensor.matmul_mx(
-                    out=acc_j[j, c][:],
-                    lhsT=g_words[a][:, 128 * j : 128 * (j + 1)].bitcast(FP8X4),
-                    lhsT_scale=g_planes[4 * a : P, 128 * j : 128 * (j + 1)],
-                    rhs=codes[1, a, part][:, 256 + 128 * c : 384 + 128 * c].bitcast(FP8X4),
-                    rhs_scale=scales[1, a, part][:, 256 + 128 * c : 384 + 128 * c],
-                    start=(a == 0 and part == "hi"),
-                    stop=(a == PASSES - 1 and part == "lo"),
+                    out=acc_n[t][:], lhsT=cols, lhsT_scale=col_scales,
+                    rhs=g_words[a][:].bitcast(FP8X4), rhs_scale=g_planes[4 * a : P, :],
+                    start=start, stop=stop,
                 )
+            else:
+                for j in range(2):
+                    nc.tensor.matmul_mx(
+                        out=acc_j[j, t - 6][:],
+                        lhsT=g_words[a][:, 128 * j : 128 * (j + 1)].bitcast(FP8X4),
+                        lhsT_scale=g_planes[4 * a : P, 128 * j : 128 * (j + 1)],
+                        rhs=cols, rhs_scale=col_scales, start=start, stop=stop,
+                    )
+
+        def flush():
+            todo = list(pending)
+            pending.clear()
+            for t, a, part in todo:
+                if a in gathered and (t in acc_n or t >= 6):
+                    multiply(t, a, part)
+                else:
+                    pending.append((t, a, part))
 
         def finish_n(t0, t1):
             yt = {}
             for t in range(t0, t1):
                 yt[t] = keep.tile([P, S], F32, name="yt%d" % t, align_bytes=64)
-                nc.scalar.activation(yt[t][:], acc_n[t][:], mybir.ActivationFunctionType.Identity, bias=b_col[:, t : t + 1])
+                nc.scalar.activation(yt[t][:], acc_n[t][:], IDENTITY, bias=b_col[:, t : t + 1])
             n = 128 * (t1 - t0)
             for j in range(2):
                 turned = psum.tile([P, n], F32, name="turned%d_%d" % (t0, j), tag="bank%d" % j)
@@ -190,65 +211,31 @@ def tile_list_tabw_tm_hl_bias_kernel(tc, tab, w, b, offs, out):
                 nc.vector.tensor_tensor(y[:], acc_j[j, c][:], bias[:, 128 * c : 128 * (c + 1)], ADD)
                 (nc.scalar if j == 1 else nc.sync).dma_start(out[128 * j : 128 * (j + 1), n0 : n0 + 128], y[:])
 
-        pending = []
-        state = {"gathered": [], "first": False}
-
-        def ready(job):
-            kind, where, a, part = job
-            return a in state["gathered"] and (kind == "j" or where < 4 or state["first"])
-
-        def flush():
-            todo = list(pending)
-            pending.clear()
-            for job in todo:
-                if ready(job):
-                    if job[0] == "n":
-                        mult_n(job[1], job[2], job[3])
-                    else:
-                        mult_j(job[1], job[2], job[3])
-                else:
-                    pending.append(job)
-
-        def mult_piece(i, part):
-            h, a, c0, wd = pieces[i]
-            for c in range(c0, c0 + wd, 128):
-                n0 = h * HALF + c
-                pending.append(("n", n0 // 128, a, part) if n0 < 768 else ("j", n0 // 128 - 6, a, part))
-            flush()
-
-        gathers = {3: 0, 4: 1, 5: 2}
+        gathers = {4: 0, 6: 1, 7: 2}
         n = len(pieces)
         for i in range(n):
+            copy_top(i)
+        for i in range(n):
+            mask_hi(i)
             if i > 0:
-                mask_hi(pieces[i])
-                if i > 1:
-                    quant(pieces[i - 1], "lo")
-                    mult_piece(i - 1, "lo")
+                quant(i - 1, "lo")
+                flush()
+            if i == 3:
+                nc.vector.tensor_copy(g_planes[:], planes[:].bitcast(U8).indirect(offsets[:]))
             if i in gathers:
                 gather_words(gathers[i])
-                state["gathered"].append(gathers[i])
                 flush()
-            if i == 2:
-                nc.vector.tensor_copy(g_planes[:], planes[:].bitcast(U8).indirect(offsets[:]))
-            if i == 7:
+            if i == 8:
                 finish_n(0, 4)
                 for t in (4, 5):
                     acc_n[t] = psum.tile([P, S], F32, name="bank_%d" % t, tag="bank%d" % (t - 2))
-                state["first"] = True
                 flush()
-            if i == 9:
+            if i == 10:
                 finish_n(4, 6)
-            sub_lo(pieces[i])
-            if i > 0:
-                quant(pieces[i], "hi")
-                mult_piece(i, "hi")
-            if i == 1:
-                quant(pieces[0], "hi")
-                mult_piece(0, "hi")
-                quant(pieces[0], "lo")
-                mult_piece(0, "lo")
-            if i == n - 1:
-                finish_j(0)
-        quant(pieces[n - 1], "lo")
-        mult_piece(n - 1, "lo")
+            sub_lo(i)
+            quant(i, "hi")
+            flush()
+        finish_j(0)
+        quant(n - 1, "lo")
+        flush()
         finish_j(1)

@@ -43,10 +43,10 @@ def tile_list_tabw_tm_hl_bias_kernel(tc, tab, w, b, offs, out):
         b_col = keep.tile([P, 6], F32, name="bcol")
         ident = keep.tile([P, P], F32, name="ident", align_bytes=64)
 
-        loads = [(0, 0, 128), (0, 128, 128), (0, 256, 256), (1, 0, 512), (2, 0, 512), (0, 512, 512), (1, 512, 512), (2, 512, 512)]
+        loads = [(0, 0, 128), (0, 128, 128), (0, 256, 256), (1, 0, 256), (1, 256, 256), (2, 0, 512), (0, 512, 512), (1, 512, 512), (2, 512, 512)]
         pieces = [
-            (0, 0, 128, True), (1, 0, 128, False), (2, 0, 256, True), (3, 0, 256, False), (3, 256, 256, False), (4, 0, 512, False),
-            (5, 0, 512, False), (6, 0, 512, False), (7, 0, 256, False), (7, 256, 128, False), (7, 384, 128, False),
+            (0, 0, 128, True), (1, 0, 128, True), (2, 0, 256, True), (3, 0, 256, True), (4, 0, 256, False), (5, 0, 512, False),
+            (6, 0, 512, False), (7, 0, 512, False), (8, 0, 256, False), (8, 256, 128, False), (8, 384, 128, False),
         ]
         raw = [keep.tile([P, PACK, wd], F32, name="raw%d" % i, align_bytes=64) for i, (a, c, wd) in enumerate(loads)]
         top = [keep.tile([P, wd, PACK], BF16, name="top%d" % i, align_bytes=64) for i, (ld, c, wd, wide) in enumerate(pieces)]
@@ -75,18 +75,19 @@ def tile_list_tabw_tm_hl_bias_kernel(tc, tab, w, b, offs, out):
         load_w(1)
         nc.sync.dma_start(offsets[:], offs)
         load_w(2)
+        load_w(3)
         for q in range(4):
             first = 512 * T + 4 * q * T
             src = tab[:, first : first + 4 * T].rearrange("a (r t) -> a r t", r=4).bitcast(I32)
             nc.sync.dma_start(planes[32 * q : 32 * q + 4 * PASSES, :], src)
-        load_w(3)
-        load_words(0)
         load_w(4)
-        load_words(1)
         load_w(5)
-        load_words(2)
+        load_words(0)
         load_w(6)
+        load_words(1)
         load_w(7)
+        load_words(2)
+        load_w(8)
         nc.sync.dma_start(b_col[:], b[0:768].rearrange("(c p) -> p c", p=P))
         nc.sync.dma_start(bias[:], b[768:1024].partition_broadcast(P))
         make_identity(nc, ident[:])
@@ -204,14 +205,14 @@ def tile_list_tabw_tm_hl_bias_kernel(tc, tab, w, b, offs, out):
                 nc.scalar.copy(y[:], turned[:])
                 nc.sync.dma_start(out[128 * j : 128 * (j + 1), 128 * t0 : 128 * t1], y[:])
 
-        def finish_j(c):
+        def finish_j(c, tokens):
             n0 = 768 + 128 * c
-            for j in range(2):
+            for j in tokens:
                 y = keep.tile([P, 128], F32, name="yj%d_%d" % (c, j), align_bytes=64)
                 nc.vector.tensor_tensor(y[:], acc_j[j, c][:], bias[:, 128 * c : 128 * (c + 1)], ADD)
                 (nc.scalar if j == 1 else nc.sync).dma_start(out[128 * j : 128 * (j + 1), n0 : n0 + 128], y[:])
 
-        gathers = {4: 0, 6: 1, 7: 2}
+        gathers = {6: (0, 1), 7: (2,)}
         n = len(pieces)
         for i in range(n):
             copy_top(i)
@@ -223,7 +224,8 @@ def tile_list_tabw_tm_hl_bias_kernel(tc, tab, w, b, offs, out):
             if i == 3:
                 nc.vector.tensor_copy(g_planes[:], planes[:].bitcast(U8).indirect(offsets[:]))
             if i in gathers:
-                gather_words(gathers[i])
+                for a in gathers[i]:
+                    gather_words(a)
                 flush()
             if i == 8:
                 finish_n(0, 4)
@@ -232,10 +234,15 @@ def tile_list_tabw_tm_hl_bias_kernel(tc, tab, w, b, offs, out):
                 flush()
             if i == 10:
                 finish_n(4, 6)
+            if i == n - 1:
+                quant(i, "hi")
+                flush()
             sub_lo(i)
-            quant(i, "hi")
-            flush()
-        finish_j(0)
+            if i < n - 1:
+                quant(i, "hi")
+                flush()
+        finish_j(0, (0,))
         quant(n - 1, "lo")
         flush()
-        finish_j(1)
+        finish_j(0, (1,))
+        finish_j(1, (0, 1))

from contextlib import ExitStack

import concourse.mybir as mybir
from concourse.masks import make_identity

K, M, T, S = 1536, 1024, 1024, 256

F32 = mybir.dt.float32
BF16 = mybir.dt.bfloat16
I32 = mybir.dt.int32
U32 = mybir.dt.uint32
U16 = mybir.dt.uint16
U8 = mybir.dt.uint8
FP8X4 = mybir.dt.float8_e4m3fn_x4
ADD = mybir.AluOpType.add
SUB = mybir.AluOpType.subtract
AND = mybir.AluOpType.bitwise_and
IDENTITY = mybir.ActivationFunctionType.Identity

FLOPS = 2 * 2 * S * K * M

P = 128
PACK = 4
PASSES = 3
HALF = 512
MASK32 = -0x00100000
MASK16 = -0x000F0010


def tile_list_tabw_tm_hl_bias_kernel(tc, tab, w, b, offs, out):
    nc = tc.nc
    with ExitStack() as ctx:
        lists = ctx.enter_context(tc.tile_pool(name="lists", bufs=1))
        keep = ctx.enter_context(tc.tile_pool(name="keep", bufs=1))
        psum = ctx.enter_context(tc.psum_pool(name="psum", bufs=1))

        offsets = lists.tile([P, S // 16], U16, name="offsets")
        words = [keep.tile([P, T], I32, name="words%d" % a, align_bytes=64) for a in range(PASSES)]
        planes = keep.tile([P, T // 4], I32, name="planes", align_bytes=64)
        g_words = [keep.tile([P, S], U32, name="gwords%d" % a, align_bytes=64) for a in range(PASSES)]
        g_planes = keep.tile([P, S], U8, name="gplanes", align_bytes=64)
        bias = keep.tile([P, 256], F32, name="bias", align_bytes=64)
        b_col = keep.tile([P, 6], F32, name="bcol")
        ident = keep.tile([P, P], F32, name="ident", align_bytes=64)

        loads = [(0, 0, 128), (0, 128, 128), (0, 256, 256), (1, 0, 256), (1, 256, 256), (2, 0, 512), (0, 512, 512), (1, 512, 512), (2, 512, 512)]
        pieces = [
            (0, 0, 128, True), (1, 0, 128, True), (2, 0, 256, True), (3, 0, 256, True), (4, 0, 256, False), (5, 0, 512, False),
            (6, 0, 512, False), (7, 0, 512, False), (8, 0, 256, False), (8, 256, 128, False), (8, 384, 128, False),
        ]
        raw = [keep.tile([P, PACK, wd], F32, name="raw%d" % i, align_bytes=64) for i, (a, c, wd) in enumerate(loads)]
        top = [keep.tile([P, wd, PACK], BF16, name="top%d" % i, align_bytes=64) for i, (ld, c, wd, wide) in enumerate(pieces)]
        hi = [keep.tile([P, wd, PACK], BF16, name="hi%d" % i, align_bytes=64) for i, (ld, c, wd, wide) in enumerate(pieces)]
        lo = [keep.tile([P, wd, PACK], BF16, name="lo%d" % i, align_bytes=64) for i, (ld, c, wd, wide) in enumerate(pieces)]
        codes = {}
        scales = {}
        for h in range(2):
            for a in range(PASSES):
                for part in ("hi", "lo"):
                    codes[h, a, part] = keep.tile([P, HALF], U32, name="codes_%s%d%d" % (part, h, a), align_bytes=64)
                    scales[h, a, part] = keep.tile([P, HALF], U8, name="scales_%s%d%d" % (part, h, a), align_bytes=64)

        def load_w(i):
            a, c, wd = loads[i]
            nc.sync.dma_start(raw[i][:], w[512 * a : 512 * (a + 1), c : c + wd].rearrange("(p j) n -> p j n", j=PACK))

        def load_words(a):
            nc.sync.dma_start(words[a][:], tab[a : a + 1, 0 : 512 * T].rearrange("o (p x) -> (o p) x", p=P).bitcast(I32))

        warm = keep.tile([P, 2], BF16, name="warm")
        nc.gpsimd.memset(warm[:], 0)
        nc.scalar.copy(warm[:, 1:2], warm[:, 0:1])
        nc.vector.memset(planes[:], 0)
        load_w(0)
        load_w(1)
        nc.sync.dma_start(offsets[:], offs)
        load_w(2)
        load_w(3)
        for q in range(4):
            first = 512 * T + 4 * q * T
            src = tab[:, first : first + 4 * T].rearrange("a (r t) -> a r t", r=4).bitcast(I32)
            nc.sync.dma_start(planes[32 * q : 32 * q + 4 * PASSES, :], src)
        load_w(4)
        load_w(5)
        load_words(0)
        load_w(6)
        load_words(1)
        load_w(7)
        load_words(2)
        load_w(8)
        nc.sync.dma_start(b_col[:], b[0:768].rearrange("(c p) -> p c", p=P))
        nc.sync.dma_start(bias[:], b[768:1024].partition_broadcast(P))
        make_identity(nc, ident[:])

        def columns(i):
            ld, c, wd, wide = pieces[i]
            return raw[ld][:, :, c : c + wd]

        def by_four(tile):
            return tile.rearrange("p (c i) j -> p c j i", i=4)

        wides = {}
        for i, (ld, c, wd, wide) in enumerate(pieces):
            if wide:
                wides[i] = keep.tile([P, PACK, wd], F32, name="wide%d" % i, align_bytes=64)

        def mask_hi(i):
            if i in wides:
                nc.vector.tensor_single_scalar(wides[i][:].bitcast(I32), columns(i).bitcast(I32), MASK32, AND)
                nc.scalar.copy(by_four(hi[i][:]), wides[i][:].rearrange("p j (c i) -> p c j i", i=4))
            else:
                nc.vector.tensor_single_scalar(
                    hi[i][:].rearrange("p n j -> p (n j)").bitcast(I32),
                    top[i][:].rearrange("p n j -> p (n j)").bitcast(I32),
                    MASK16,
                    AND,
                )

        def copy_top(i):
            ld, c0, wd, wide = pieces[i]
            if not wide:
                src = raw[ld][:].bitcast(BF16).rearrange("p j (c i u) -> p c j i u", i=4, u=2)
                dst = by_four(top[i][:])
                step = min(64, wd // 4)
                for c in range(0, wd // 4, step):
                    nc.scalar.copy(dst[:, c : c + step], src[:, c0 // 4 + c : c0 // 4 + c + step, :, :, 1])

        def sub_lo(i):
            high = wides[i][:].rearrange("p j (c i) -> p c j i", i=4) if i in wides else by_four(hi[i][:])
            nc.vector.tensor_tensor(by_four(lo[i][:]), columns(i).rearrange("p j (c i) -> p c j i", i=4), high, SUB)

        def place(i):
            ld, c, wd, wide = pieces[i]
            a, n0, lw = loads[ld]
            return a, n0 + c, wd

        def quant(i, part):
            a, n0, wd = place(i)
            h, c = divmod(n0, HALF)
            src = hi[i] if part == "hi" else lo[i]
            nc.vector.quantize_mx(
                out=codes[h, a, part][:, c : c + wd].bitcast(FP8X4),
                scales=scales[h, a, part][:, c : c + wd],
                in_=src[:].rearrange("p n j -> p (n j)"),
            )
            for n in range(n0, n0 + wd, 128):
                pending.append((n // 128, a, part))

        def gather_words(a):
            nc.vector.tensor_copy(g_words[a][:], words[a][:].bitcast(U32).indirect(offsets[:]))
            gathered.append(a)

        acc_n = {}
        acc_j = {}
        for t in range(4):
            acc_n[t] = psum.tile([P, S], F32, name="bank%d" % t, tag="bank%d" % t)
        for j in range(2):
            for c in range(2):
                acc_j[j, c] = psum.tile([P, 128], F32, name="accj%d%d" % (j, c))

        pending = []
        gathered = []

        def multiply(t, a, part):
            h, c = t // 4, 128 * (t % 4)
            cols = codes[h, a, part][:, c : c + 128].bitcast(FP8X4)
            col_scales = scales[h, a, part][:, c : c + 128]
            start = a == 0 and part == "hi"
            stop = a == PASSES - 1 and part == "lo"
            if t < 6:
                nc.tensor.matmul_mx(
                    out=acc_n[t][:], lhsT=cols, lhsT_scale=col_scales,
                    rhs=g_words[a][:].bitcast(FP8X4), rhs_scale=g_planes[4 * a : P, :],
                    start=start, stop=stop,
                )
            else:
                for j in range(2):
                    nc.tensor.matmul_mx(
                        out=acc_j[j, t - 6][:],
                        lhsT=g_words[a][:, 128 * j : 128 * (j + 1)].bitcast(FP8X4),
                        lhsT_scale=g_planes[4 * a : P, 128 * j : 128 * (j + 1)],
                        rhs=cols, rhs_scale=col_scales, start=start, stop=stop,
                    )

        def flush():
            todo = list(pending)
            pending.clear()
            for t, a, part in todo:
                if a in gathered and (t in acc_n or t >= 6):
                    multiply(t, a, part)
                else:
                    pending.append((t, a, part))

        def finish_n(t0, t1):
            yt = {}
            for t in range(t0, t1):
                yt[t] = keep.tile([P, S], F32, name="yt%d" % t, align_bytes=64)
                nc.scalar.activation(yt[t][:], acc_n[t][:], IDENTITY, bias=b_col[:, t : t + 1])
            n = 128 * (t1 - t0)
            for j in range(2):
                turned = psum.tile([P, n], F32, name="turned%d_%d" % (t0, j), tag="bank%d" % j)
                for t in range(t0, t1):
                    nc.tensor.transpose(turned[:, 128 * (t - t0) : 128 * (t - t0 + 1)], yt[t][:, 128 * j : 128 * (j + 1)], ident[:])
                y = keep.tile([P, n], F32, name="y%d_%d" % (t0, j), align_bytes=64)
                nc.scalar.copy(y[:], turned[:])
                nc.sync.dma_start(out[128 * j : 128 * (j + 1), 128 * t0 : 128 * t1], y[:])

        def finish_j(c, tokens):
            n0 = 768 + 128 * c
            for j in tokens:
                y = keep.tile([P, 128], F32, name="yj%d_%d" % (c, j), align_bytes=64)
                nc.vector.tensor_tensor(y[:], acc_j[j, c][:], bias[:, 128 * c : 128 * (c + 1)], ADD)
                (nc.scalar if j == 1 else nc.sync).dma_start(out[128 * j : 128 * (j + 1), n0 : n0 + 128], y[:])

        gathers = {6: (0, 1), 7: (2,)}
        n = len(pieces)
        for i in range(n):
            copy_top(i)
        for i in range(n):
            mask_hi(i)
            if i > 0:
                quant(i - 1, "lo")
                flush()
            if i == 3:
                nc.vector.tensor_copy(g_planes[:], planes[:].bitcast(U8).indirect(offsets[:]))
            if i in gathers:
                for a in gathers[i]:
                    gather_words(a)
                flush()
            if i == 8:
                finish_n(0, 4)
                for t in (4, 5):
                    acc_n[t] = psum.tile([P, S], F32, name="bank_%d" % t, tag="bank%d" % (t - 2))
                flush()
            if i == 10:
                finish_n(4, 6)
            if i == n - 1:
                quant(i, "hi")
                flush()
            sub_lo(i)
            if i < n - 1:
                quant(i, "hi")
                flush()
        finish_j(0, (0,))
        quant(n - 1, "lo")
        flush()
        finish_j(0, (1,))
        finish_j(1, (0, 1))
